import numpy as np
import ml_dtypes


def mxq(x, axis, fmt="e4m3"):
    dtype, down = {"e4m3": (ml_dtypes.float8_e4m3fn, 7), "e5m2": (ml_dtypes.float8_e5m2, 14)}[fmt]
    v = np.moveaxis(np.asarray(x, np.float32).astype(ml_dtypes.bfloat16).astype(np.float64), axis, -1)
    blocks = v.reshape(v.shape[:-1] + (-1, 32))
    amax = np.abs(blocks).max(-1, keepdims=True)
    byte = np.maximum(np.where(amax > 0, np.frexp(amax)[1] - 1 + 127, 0) - down, 1)
    scale = np.exp2(byte - 127.0)
    codes = (blocks / scale).astype(np.float32).astype(dtype).astype(np.float64)
    return np.moveaxis((codes * scale).reshape(v.shape), -1, axis)


WIDE = False


def mx_kscale(k):
    if not WIDE:
        return np.ones(k)
    levels = np.array([10, -10, 5, -5, 0])
    if k % 512:
        return np.exp2(np.random.permutation(np.resize(levels, k // 32))).repeat(32)
    a = np.empty((k // 512, 16))
    for p in range(k // 512):
        a[p, :8] = np.random.permutation(np.resize(levels, 8))
        for g in range(8):
            far = levels[np.abs(levels - a[p, g]) >= 10]
            a[p, g + 8] = far[np.random.randint(len(far))]
    return np.exp2(a.ravel()).repeat(32)


def f64(x):
    return np.asarray(x).astype(np.float64)


def striped(idx):
    return np.tile(np.asarray(idx).reshape(-1, 16).T, (8, 1)).astype(np.uint16)


def unstriped(offs):
    return offs[:16].T.reshape(-1).astype(np.int64)


E2M1 = np.array([0.0, 0.5, 1.0, 1.5, 2.0, 3.0, 4.0, 6.0, -0.0, -0.5, -1.0, -1.5, -2.0, -3.0, -4.0, -6.0])


def pack_weight(w, fmt):
    k, n = w.shape
    w = f64(np.asarray(w, np.float32).astype(ml_dtypes.bfloat16)).reshape(k // 32, 32, n)
    amax = np.abs(w).max(1)
    if fmt == "e4m3":
        byte = np.frexp(amax)[1] - 1 + 127 - 7
    else:
        mant, ex = np.frexp(amax / 6.0)
        byte = np.where(mant > 0.5, ex, ex - 1) + 127
    byte = np.clip(np.where(amax > 0, byte, 1), 1, 254)
    scaled = (w * np.exp2(127.0 - byte)[:, None, :]).reshape(k, n).astype(np.float32)
    by_word = np.ascontiguousarray(scaled.reshape(k // 512, 128, 4, n).transpose(0, 1, 3, 2))
    if fmt == "e4m3":
        words = by_word.astype(ml_dtypes.float8_e4m3fn).view(np.uint8)
    else:
        c = by_word.astype(ml_dtypes.float4_e2m1fn).view(np.uint8) & 0xF
        words = (c[..., 0::2] | (c[..., 1::2] << 4)).reshape(k // 512, 128, 2 * n)
    return np.ascontiguousarray(words), np.ascontiguousarray(byte.astype(np.uint8).reshape(k // 512, 16, n))


def unpack_weight(words, scales, fmt):
    g, _, n = scales.shape
    words = np.ascontiguousarray(words).reshape(g, 128, n, -1)
    if fmt == "e4m3":
        vals = words.view(ml_dtypes.float8_e4m3fn).astype(np.float64)
    else:
        nib = np.empty((g, 128, n, 4), np.uint8)
        nib[..., 0::2] = words & 0xF
        nib[..., 1::2] = words >> 4
        vals = E2M1[nib]
    vals = vals * np.repeat(np.exp2(scales.astype(np.float64) - 127.0), 8, axis=1)[..., None]
    return vals.transpose(0, 1, 3, 2).reshape(g * 512, n)


def bf(x):
    return np.asarray(x, np.float32).astype(ml_dtypes.bfloat16)


def planes(Y):
    r, m = Y.shape
    b = f64(bf(Y)).reshape(r // 32, 32, m)
    amax = np.abs(b).max(1)
    byte = np.clip(np.where(amax > 0, np.frexp(amax)[1] - 1 + 127 - 7, 1), 1, 254)
    codes = (b * np.exp2(127.0 - byte)[:, None, :]).reshape(r, m).astype(np.float32).astype(ml_dtypes.float8_e4m3fn).view(np.uint8)
    words = codes.reshape(r // 512, 128, 4, m).transpose(0, 1, 3, 2)
    return np.ascontiguousarray(words), np.ascontiguousarray(byte.astype(np.uint8).reshape(r // 512, 16, m))


D, T, I, Q, E = 512, 2048, 512, 256, 512


def setup_inputs():
    n = np.random.standard_normal
    idx = np.random.permutation(T)[:I]
    idx2 = np.random.permutation(T)[:I]
    idx3 = np.random.permutation(T)[:I]
    fd = mx_kscale(D)
    fi = mx_kscale(I)
    ti = np.ones(T)
    ti[idx] = fi
    keysp = pack_weight(n((D, T)) / fd[:, None], "e2m1")
    return {
        "query": (n((D, Q)) * 0.9 / np.sqrt(D) * fd[:, None]).astype(np.float32),
        "keys_words": keysp[0],
        "keys_scales": keysp[1],
        "lam": (np.random.uniform(0.3, 0.9, (Q, 1))).astype(np.float32),
        "os": (np.random.uniform(0.02, 0.08, (1, I)) * fi).astype(np.float32),
        "vals": (n((E, T)) / ti).astype(np.float32),
        "offs": striped(idx),
        "offs2": striped(idx2),
        "offs3": striped(idx3),
    }


def reference(query, keys_words, keys_scales, lam, os, vals, offs, offs2, offs3):
    idx = unstriped(offs)
    idx2 = unstriped(offs2)
    idx3 = unstriped(offs3)
    keysu = unpack_weight(keys_words, keys_scales, "e2m1")
    queryq = mxq(f64(query), 0, "e4m3")
    a = queryq.T @ keysu
    s = a[:, idx] + np.maximum(a[:, idx2], a[:, idx3]) * f64(lam)
    w = np.maximum(s, 0.0)
    wo1 = w * f64(os)
    wt1 = wo1.T
    vt1 = f64(vals)[:, idx].T
    vt1q = mxq(vt1, 0, "e4m3")
    wt1q = mxq(wt1, 0, "e4m3")
    o = vt1q.T @ wt1q
    words, scales = planes(o)
    return o, words, scales

@@ -1,0 +1,200 @@
+from contextlib import ExitStack
+
+import concourse.mybir as mybir
+from concourse.masks import make_identity
+
+D, T, I, Q, E = 512, 2048, 512, 256, 512
+FLOPS = 2 * D * Q * T + 2 * I * E * Q
+
+F32 = mybir.dt.float32
+BF16 = mybir.dt.bfloat16
+I32 = mybir.dt.int32
+U32 = mybir.dt.uint32
+U16 = mybir.dt.uint16
+U8 = mybir.dt.uint8
+FP8X4 = mybir.dt.float8_e4m3fn_x4
+FP4X4 = mybir.dt.float4_e2m1fn_x4
+ALU = mybir.AluOpType
+COPY = mybir.ActivationFunctionType.Copy
+
+P = 128
+PACK = 4
+BANK = 512
+QB = Q // P
+CHUNKS = T // BANK
+
+
+def tile_attend_lookahead_read_lean_pl_kernel(
+    tc, query, keys_words, keys_scales, lam, slot_factor, vals, offs, offs2, offs3, out_0, out_1, out_2
+):
+    nc = tc.nc
+    with ExitStack() as ctx:
+        sb = ctx.enter_context(tc.tile_pool(name="sb", bufs=1))
+        psum = ctx.enter_context(tc.psum_pool(name="psum", bufs=7))
+        psum_late = ctx.enter_context(tc.psum_pool(name="psum_late", bufs=1))
+
+        list1 = sb.tile([P, I // 16], U16, name="list1")
+        list2 = sb.tile([P, I // 16], U16, name="list2")
+        list3 = sb.tile([P, I // 16], U16, name="list3")
+        q_raw = sb.tile([P, PACK, Q], F32, name="q_raw")
+        k_words = [sb.tile([P, T], U8, name=f"k_words{h}", align_bytes=64) for h in range(2)]
+        k_scales = sb.tile([P, T], U8, name="k_scales", align_bytes=64)
+        lam_sb = sb.tile([P, QB], F32, name="lam_sb")
+        os_sb = sb.tile([P, PACK], F32, name="os_sb")
+        ident = sb.tile([P, P], F32, name="ident")
+        v_pool = [sb.tile([P, T], F32, name=f"v_pool{t}") for t in range(PACK)]
+        a_sb = [sb.tile([P, T], F32, name=f"a_sb{b}") for b in range(QB)]
+
+        nc.vector.memset(k_scales[:].bitcast(I32), 0)
+        vals_planes = vals.rearrange("(p t) c -> p t c", t=PACK)
+        nc.sync.dma_start(out=q_raw[:], in_=query.rearrange("(p j) q -> p j q", j=PACK))
+        nc.sync.dma_start(out=k_words[0][:].bitcast(I32), in_=keys_words[0, :, :T].bitcast(I32))
+        nc.sync.dma_start(list2[:], offs2)
+        for quad in range(4):
+            nc.sync.dma_start(
+                out=k_scales[32 * quad : 32 * quad + 4, :].bitcast(I32),
+                in_=keys_scales[0, 4 * quad : 4 * quad + 4, :].bitcast(I32),
+            )
+        nc.sync.dma_start(out=k_words[1][:].bitcast(I32), in_=keys_words[0, :, T:].bitcast(I32))
+        nc.sync.dma_start(out=v_pool[0][:], in_=vals_planes[:, 0, :])
+        nc.sync.dma_start(list1[:], offs)
+        nc.sync.dma_start(list3[:], offs3)
+        with nc.allow_non_contiguous_dma(reason="one factor a query row, rows on the partitions"):
+            nc.sync.dma_start(out=lam_sb[:], in_=lam.rearrange("(b p) o -> p (b o)", p=P))
+        nc.sync.dma_start(out=os_sb[:], in_=slot_factor.rearrange("o (p r) -> p (o r)", r=PACK))
+        for t in range(1, PACK):
+            nc.sync.dma_start(out=v_pool[t][:], in_=vals_planes[:, t, :])
+        make_identity(nc, ident[:])
+
+        def quantize(name, grouped, width):
+            codes = sb.tile([P, width], U32, name=name + "_codes", align_bytes=64)
+            scales = sb.tile([P, width], U8, name=name + "_scales", align_bytes=64)
+            nc.vector.quantize_mx(out=codes[:].bitcast(FP8X4), scales=scales[:], in_=grouped)
+            return codes, scales
+
+        def gather(engine, dst, window, offsets):
+            if engine == "vector":
+                nc.vector.tensor_copy(dst, window[:].indirect(offsets[:]))
+            else:
+                nc.scalar.activation(dst, window[:].indirect(offsets[:]), COPY)
+
+        q_grouped = [sb.tile([P, P, PACK], BF16, name=f"q_grouped{b}", align_bytes=64) for b in range(QB)]
+        q_view = q_raw[:].rearrange("p j q -> p q j")
+        nc.vector.tensor_copy(out=q_grouped[0][:], in_=q_view[:, 0:P, :])
+        nc.scalar.copy(out=q_grouped[1][:], in_=q_view[:, P : 2 * P, :])
+        q_mx = [quantize(f"q{b}", q_grouped[b][:].rearrange("p q j -> p (q j)"), P) for b in range(QB)]
+
+        a_bank = {}
+        for b in range(QB):
+            for c in range(CHUNKS):
+                a_bank[b, c] = psum.tile([P, BANK], F32, name="bank")
+                first = 2 * BANK * (c % 2)
+                nc.tensor.matmul_mx(
+                    out=a_bank[b, c][:],
+                    lhsT=q_mx[b][0][:].bitcast(FP8X4),
+                    lhsT_scale=q_mx[b][1][:],
+                    rhs=k_words[c // 2][:, first : first + 2 * BANK].bitcast(FP4X4),
+                    rhs_scale=k_scales[:, BANK * c : BANK * (c + 1)],
+                    start=True,
+                    stop=True,
+                )
+                nc.scalar.copy(out=a_sb[b][:, BANK * c : BANK * (c + 1)], in_=a_bank[b, c][:])
+
+        token, follow2, follow3, larger, s_sb = (
+            [sb.tile([P, I], F32, name=f"{name}{b}", align_bytes=64) for b in range(QB)]
+            for name in ("token", "follow2_", "follow3_", "larger", "s_sb")
+        )
+        w_bank = {}
+
+        def turn_values(engine, t, pairs, bank):
+            gather(engine, pairs.bitcast(BF16), v_pool[t], list1)
+            for u in range(2):
+                nc.tensor.transpose(bank[:, u, :], pairs[:, u::2], ident[:])
+
+        def turn_scores(b):
+            nc.vector.scalar_tensor_tensor(
+                s_sb[b][:], larger[b][:], lam_sb[:, b : b + 1], token[b][:], ALU.mult, ALU.add
+            )
+            w_bank[b] = psum.tile([P, PACK, P], F32, name="bank")
+            for r in range(PACK):
+                nc.tensor.transpose(w_bank[b][:, r, :], s_sb[b][:, r::PACK], ident[:])
+
+        def weigh(b, grouped):
+            nc.vector.scalar_tensor_tensor(
+                grouped.rearrange("p (q r) -> p q r", r=PACK),
+                w_bank[b][:].rearrange("p r q -> p q r"),
+                0.0,
+                os_sb[:].unsqueeze(1).to_broadcast([P, P, PACK]),
+                ALU.max,
+                ALU.mult,
+            )
+
+        v_pairs = [sb.tile([P, I // 2], F32, name=f"v_pairs{t}") for t in (0, 2, 3)]
+        v_grouped = [
+            sb.tile([P, n * P * PACK], BF16, name=f"v_grouped{t}", align_bytes=64) for t, n in ((0, 1), (1, 1), (2, 2))
+        ]
+
+        v_bank0 = psum.tile([P, 2, P], F32, name="bank")
+        turn_values("vector", 0, v_pairs[0][:], v_bank0)
+        gather("vector", follow2[0][:], a_sb[0], list2)
+        gather("vector", follow3[0][:], a_sb[0], list3)
+        nc.vector.tensor_tensor(larger[0][:], follow2[0][:], follow3[0][:], ALU.max)
+        gather("vector", token[0][:], a_sb[0], list1)
+        turn_scores(0)
+        gather("scalar", follow2[1][:], a_sb[1], list2)
+        gather("scalar", follow3[1][:], a_sb[1], list3)
+        nc.scalar.copy(out=v_grouped[0][:].bitcast(F32), in_=v_bank0[:].rearrange("p u e -> p e u"))
+        gather("scalar", token[1][:], a_sb[1], list1)
+        nc.vector.tensor_tensor(larger[1][:], follow2[1][:], follow3[1][:], ALU.max)
+        v_mx0 = quantize("v0", v_grouped[0][:], P)
+        turn_scores(1)
+        v_bank1 = psum.tile([P, 2, P], F32, name="bank")
+        turn_values("vector", 1, larger[1][:, : I // 2], v_bank1)
+        v_bank23 = psum_late.tile([P, 2, 2, P], F32, name="v_bank23", tag="late")
+        turn_values("scalar", 2, v_pairs[1][:], v_bank23[:, 0])
+        turn_values("scalar", 3, v_pairs[2][:], v_bank23[:, 1])
+        w_grouped = [follow3[1][:, : I // 2].bitcast(BF16), follow2[1][:, : I // 2].bitcast(BF16)]
+        weigh(0, w_grouped[0])
+        w_mx0 = quantize("w0", w_grouped[0], P)
+        weigh(1, w_grouped[1])
+        nc.vector.tensor_copy(out=v_grouped[1][:].bitcast(F32), in_=v_bank1[:].rearrange("p u e -> p e u"))
+        w_mx1 = quantize("w1", w_grouped[1], P)
+        v_mx1 = quantize("v1", v_grouped[1][:], P)
+        nc.scalar.copy(out=v_grouped[2][:].bitcast(F32), in_=v_bank23[:].rearrange("p t u e -> p t e u"))
+        v_mx23 = quantize("v23", v_grouped[2][:], 2 * P)
+        w_mx = [w_mx0, w_mx1]
+        v_mx = [(v_mx0, 0), (v_mx1, 0), (v_mx23, 0), (v_mx23, P)]
+
+        o_bank = [
+            psum_late.tile([P, PACK, P], F32, name="o_bank0", tag="late"),
+            psum.tile([P, PACK, P], F32, name="bank"),
+        ]
+        for b in range(QB):
+            for t in range(PACK):
+                (codes, scales), first = v_mx[t]
+                nc.tensor.matmul_mx(
+                    out=o_bank[b][:, t, :],
+                    lhsT=codes[:, first : first + P].bitcast(FP8X4),
+                    lhsT_scale=scales[:, first : first + P],
+                    rhs=w_mx[b][0][:].bitcast(FP8X4),
+                    rhs_scale=w_mx[b][1][:],
+                    start=True,
+                    stop=True,
+                )
+
+        out_planes = out_0.rearrange("(p t) q -> p t q", t=PACK)
+        o_grouped = sb.tile([P, Q, PACK], BF16, name="o_grouped", align_bytes=64)
+        for b in range(QB):
+            cols = slice(P * b, P * (b + 1))
+            nc.vector.tensor_copy(out=o_grouped[:, cols, :], in_=o_bank[b][:].rearrange("p t q -> p q t"))
+            o_sb = sb.tile([P, PACK, P], F32, name=f"o_sb{b}")
+            nc.scalar.copy(out=o_sb[:], in_=o_bank[b][:])
+            nc.sync.dma_start(out=out_planes[:, :, cols], in_=o_sb[:])
+        o_codes, o_scales = quantize("o", o_grouped[:].rearrange("p q t -> p (q t)"), Q)
+        nc.sync.dma_start(out=out_1[0].rearrange("p c r -> p (c r)").bitcast(I32), in_=o_codes[:].bitcast(I32))
+        for quad in range(4):
+            queue = nc.scalar if quad % 2 == 0 else nc.sync
+            queue.dma_start(
+                out=out_2[0, 4 * quad : 4 * quad + 4, :].bitcast(I32),
+                in_=o_scales[32 * quad : 32 * quad + 4, :].bitcast(I32),
+            )

@@ -50,24 +50,24 @@ def tile_attend_lookahead_read_lean_pl_kernel(
         nc.sync.dma_start(out=q_raw[:], in_=query.rearrange("(p j) q -> p j q", j=PACK))
         nc.sync.dma_start(out=k_words[0][:].bitcast(I32), in_=keys_words[0, :, :T].bitcast(I32))
         nc.sync.dma_start(list2[:], offs2)
-        for quad in range(4):
+        for row in range(4):
             nc.sync.dma_start(
-                out=k_scales[32 * quad : 32 * quad + 4, :].bitcast(I32),
-                in_=keys_scales[0, 4 * quad : 4 * quad + 4, :].bitcast(I32),
+                out=k_scales[row:P:32, :].bitcast(I32), in_=keys_scales[0, row:16:4, :].bitcast(I32)
             )
         nc.sync.dma_start(out=k_words[1][:].bitcast(I32), in_=keys_words[0, :, T:].bitcast(I32))
         nc.sync.dma_start(out=v_pool[0][:], in_=vals_planes[:, 0, :])
-        nc.sync.dma_start(list1[:], offs)
         nc.sync.dma_start(list3[:], offs3)
+        nc.sync.dma_start(list1[:], offs)
         with nc.allow_non_contiguous_dma(reason="one factor a query row, rows on the partitions"):
             nc.sync.dma_start(out=lam_sb[:], in_=lam.rearrange("(b p) o -> p (b o)", p=P))
         nc.sync.dma_start(out=os_sb[:], in_=slot_factor.rearrange("o (p r) -> p (o r)", r=PACK))
         for t in range(1, PACK):
             nc.sync.dma_start(out=v_pool[t][:], in_=vals_planes[:, t, :])
-        make_identity(nc, ident[:])
+        nc.vector.memset(ident[:], 0.0)
+        make_identity(nc, ident[:], nomemset=True)
 
-        def quantize(name, grouped, width):
-            codes = sb.tile([P, width], U32, name=name + "_codes", align_bytes=64)
+        def quantize(name, grouped, width, tag=""):
+            codes = sb.tile([P, width], U32, name=name + "_codes", tag=tag, align_bytes=64)
             scales = sb.tile([P, width], U8, name=name + "_scales", align_bytes=64)
             nc.vector.quantize_mx(out=codes[:].bitcast(FP8X4), scales=scales[:], in_=grouped)
             return codes, scales
@@ -98,7 +98,11 @@ def tile_attend_lookahead_read_lean_pl_kernel(
                     start=True,
                     stop=True,
                 )
-                nc.scalar.copy(out=a_sb[b][:, BANK * c : BANK * (c + 1)], in_=a_bank[b, c][:])
+                dst = a_sb[b][:, BANK * c : BANK * (c + 1)]
+                if c % 2 == 1 and (b, c) != (QB - 1, CHUNKS - 1):
+                    nc.vector.tensor_copy(out=dst, in_=a_bank[b, c][:])
+                else:
+                    nc.scalar.copy(out=dst, in_=a_bank[b, c][:])
 
         token, follow2, follow3, larger, s_sb = (
             [sb.tile([P, I], F32, name=f"{name}{b}", align_bytes=64) for b in range(QB)]
@@ -129,13 +133,6 @@ def tile_attend_lookahead_read_lean_pl_kernel(
                 ALU.mult,
             )
 
-        v_pairs = [sb.tile([P, I // 2], F32, name=f"v_pairs{t}") for t in (0, 2, 3)]
-        v_grouped = [
-            sb.tile([P, n * P * PACK], BF16, name=f"v_grouped{t}", align_bytes=64) for t, n in ((0, 1), (1, 1), (2, 2))
-        ]
-
-        v_bank0 = psum.tile([P, 2, P], F32, name="bank")
-        turn_values("vector", 0, v_pairs[0][:], v_bank0)
         gather("vector", follow2[0][:], a_sb[0], list2)
         gather("vector", follow3[0][:], a_sb[0], list3)
         nc.vector.tensor_tensor(larger[0][:], follow2[0][:], follow3[0][:], ALU.max)
@@ -143,27 +140,29 @@ def tile_attend_lookahead_read_lean_pl_kernel(
         turn_scores(0)
         gather("scalar", follow2[1][:], a_sb[1], list2)
         gather("scalar", follow3[1][:], a_sb[1], list3)
-        nc.scalar.copy(out=v_grouped[0][:].bitcast(F32), in_=v_bank0[:].rearrange("p u e -> p e u"))
         gather("scalar", token[1][:], a_sb[1], list1)
         nc.vector.tensor_tensor(larger[1][:], follow2[1][:], follow3[1][:], ALU.max)
-        v_mx0 = quantize("v0", v_grouped[0][:], P)
         turn_scores(1)
-        v_bank1 = psum.tile([P, 2, P], F32, name="bank")
-        turn_values("vector", 1, larger[1][:, : I // 2], v_bank1)
+
+        v_pairs = [sb.tile([P, I // 2], F32, name=f"v_pairs{t}", tag=f"v_pairs{t}", align_bytes=64) for t in (1, 2, 3)]
+        v_bank01 = psum.tile([P, 2, 2, P], F32, name="bank")
+        turn_values("vector", 0, follow2[1][:, : I // 2], v_bank01[:, 0])
+        turn_values("scalar", 1, v_pairs[0][:], v_bank01[:, 1])
         v_bank23 = psum_late.tile([P, 2, 2, P], F32, name="v_bank23", tag="late")
         turn_values("scalar", 2, v_pairs[1][:], v_bank23[:, 0])
         turn_values("scalar", 3, v_pairs[2][:], v_bank23[:, 1])
-        w_grouped = [follow3[1][:, : I // 2].bitcast(BF16), follow2[1][:, : I // 2].bitcast(BF16)]
+        w_grouped = [follow3[1][:, : I // 2].bitcast(BF16), larger[1][:, : I // 2].bitcast(BF16)]
+        v_grouped = [sb.tile([P, 2 * P * PACK], BF16, name=f"v_grouped{h}", align_bytes=64) for h in range(2)]
         weigh(0, w_grouped[0])
-        w_mx0 = quantize("w0", w_grouped[0], P)
         weigh(1, w_grouped[1])
-        nc.vector.tensor_copy(out=v_grouped[1][:].bitcast(F32), in_=v_bank1[:].rearrange("p u e -> p e u"))
-        w_mx1 = quantize("w1", w_grouped[1], P)
-        v_mx1 = quantize("v1", v_grouped[1][:], P)
-        nc.scalar.copy(out=v_grouped[2][:].bitcast(F32), in_=v_bank23[:].rearrange("p t u e -> p t e u"))
-        v_mx23 = quantize("v23", v_grouped[2][:], 2 * P)
+        w_mx0 = quantize("w0", w_grouped[0], P)
+        nc.vector.tensor_copy(out=v_grouped[0][:].bitcast(F32), in_=v_bank01[:].rearrange("p t u e -> p t e u"))
+        w_mx1 = quantize("w1", w_grouped[1], P, tag="v_pairs3")
+        v_mx01 = quantize("v01", v_grouped[0][:], 2 * P)
+        nc.scalar.copy(out=v_grouped[1][:].bitcast(F32), in_=v_bank23[:].rearrange("p t u e -> p t e u"))
+        v_mx23 = quantize("v23", v_grouped[1][:], 2 * P)
         w_mx = [w_mx0, w_mx1]
-        v_mx = [(v_mx0, 0), (v_mx1, 0), (v_mx23, 0), (v_mx23, P)]
+        v_mx = [(v_mx01, 0), (v_mx01, P), (v_mx23, 0), (v_mx23, P)]
 
         o_bank = [
             psum_late.tile([P, PACK, P], F32, name="o_bank0", tag="late"),
@@ -184,17 +183,28 @@ def tile_attend_lookahead_read_lean_pl_kernel(
 
         out_planes = out_0.rearrange("(p t) q -> p t q", t=PACK)
         o_grouped = sb.tile([P, Q, PACK], BF16, name="o_grouped", align_bytes=64)
-        for b in range(QB):
+        o_sb = [sb.tile([P, PACK, P], F32, name=f"o_sb{b}") for b in range(QB)]
+        o_codes = sb.tile([P, Q], U32, name="o_codes", align_bytes=64)
+        o_scales = sb.tile([P, Q], U8, name="o_scales", align_bytes=64)
+
+        def store_result(b):
+            nc.scalar.copy(out=o_sb[b][:], in_=o_bank[b][:])
+            nc.sync.dma_start(out=out_planes[:, :, P * b : P * (b + 1)], in_=o_sb[b][:])
+
+        def quantize_result(b, source):
             cols = slice(P * b, P * (b + 1))
-            nc.vector.tensor_copy(out=o_grouped[:, cols, :], in_=o_bank[b][:].rearrange("p t q -> p q t"))
-            o_sb = sb.tile([P, PACK, P], F32, name=f"o_sb{b}")
-            nc.scalar.copy(out=o_sb[:], in_=o_bank[b][:])
-            nc.sync.dma_start(out=out_planes[:, :, cols], in_=o_sb[:])
-        o_codes, o_scales = quantize("o", o_grouped[:].rearrange("p q t -> p (q t)"), Q)
-        nc.sync.dma_start(out=out_1[0].rearrange("p c r -> p (c r)").bitcast(I32), in_=o_codes[:].bitcast(I32))
-        for quad in range(4):
-            queue = nc.scalar if quad % 2 == 0 else nc.sync
-            queue.dma_start(
-                out=out_2[0, 4 * quad : 4 * quad + 4, :].bitcast(I32),
-                in_=o_scales[32 * quad : 32 * quad + 4, :].bitcast(I32),
+            nc.vector.tensor_copy(out=o_grouped[:, cols, :], in_=source[:].rearrange("p t q -> p q t"))
+            nc.vector.quantize_mx(
+                out=o_codes[:, cols].bitcast(FP8X4),
+                scales=o_scales[:, cols],
+                in_=o_grouped[:, cols, :].rearrange("p q t -> p (q t)"),
             )
+
+        quantize_result(0, o_bank[0])
+        store_result(1)
+        store_result(0)
+        quantize_result(1, o_sb[1])
+        nc.sync.dma_start(out=out_1[0].rearrange("p c r -> p (c r)").bitcast(I32), in_=o_codes[:].bitcast(I32))
+        for row in range(4):
+            queue = nc.scalar if row % 2 == 0 else nc.sync
+            queue.dma_start(out=out_2[0, row:16:4, :].bitcast(I32), in_=o_scales[row:P:32, :].bitcast(I32))

@@ -30,16 +30,16 @@ def tile_attend_lookahead_read_lean_pl_kernel(
     nc = tc.nc
     with ExitStack() as ctx:
         sb = ctx.enter_context(tc.tile_pool(name="sb", bufs=1))
-        psum = ctx.enter_context(tc.psum_pool(name="psum", bufs=7))
-        psum_late = ctx.enter_context(tc.psum_pool(name="psum_late", bufs=1))
+        psum = ctx.enter_context(tc.psum_pool(name="psum", bufs=8))
 
         list1 = sb.tile([P, I // 16], U16, name="list1")
         list2 = sb.tile([P, I // 16], U16, name="list2")
         list3 = sb.tile([P, I // 16], U16, name="list3")
         q_raw = sb.tile([P, PACK, Q], F32, name="q_raw")
-        k_words = [sb.tile([P, T], U8, name=f"k_words{h}", align_bytes=64) for h in range(2)]
+        k_first = sb.tile([P, 2 * BANK], U8, name="k_first", align_bytes=64)
+        k_rest = sb.tile([P, 2 * (T - BANK)], U8, name="k_rest", align_bytes=64)
         k_scales = sb.tile([P, T], U8, name="k_scales", align_bytes=64)
-        lam_sb = sb.tile([P, QB], F32, name="lam_sb")
+        lam_rows = sb.tile([P, P], F32, name="lam_rows")
         os_sb = sb.tile([P, PACK], F32, name="os_sb")
         ident = sb.tile([P, P], F32, name="ident")
         v_pool = [sb.tile([P, T], F32, name=f"v_pool{t}") for t in range(PACK)]
@@ -48,20 +48,21 @@ def tile_attend_lookahead_read_lean_pl_kernel(
         nc.vector.memset(k_scales[:].bitcast(I32), 0)
         vals_planes = vals.rearrange("(p t) c -> p t c", t=PACK)
         nc.sync.dma_start(out=q_raw[:], in_=query.rearrange("(p j) q -> p j q", j=PACK))
-        nc.sync.dma_start(out=k_words[0][:].bitcast(I32), in_=keys_words[0, :, :T].bitcast(I32))
+        nc.sync.dma_start(out=k_first[:].bitcast(I32), in_=keys_words[0, :, : 2 * BANK].bitcast(I32))
         nc.sync.dma_start(list2[:], offs2)
         for row in range(4):
             nc.sync.dma_start(
                 out=k_scales[row:P:32, :].bitcast(I32), in_=keys_scales[0, row:16:4, :].bitcast(I32)
             )
-        nc.sync.dma_start(out=k_words[1][:].bitcast(I32), in_=keys_words[0, :, T:].bitcast(I32))
+        nc.sync.dma_start(out=k_rest[:].bitcast(I32), in_=keys_words[0, :, 2 * BANK :].bitcast(I32))
         nc.sync.dma_start(out=v_pool[0][:], in_=vals_planes[:, 0, :])
         nc.sync.dma_start(list3[:], offs3)
         nc.sync.dma_start(list1[:], offs)
-        with nc.allow_non_contiguous_dma(reason="one factor a query row, rows on the partitions"):
-            nc.sync.dma_start(out=lam_sb[:], in_=lam.rearrange("(b p) o -> p (b o)", p=P))
+        nc.vector.memset(lam_rows[:], 0.0)
+        nc.sync.dma_start(out=lam_rows[:QB, :], in_=lam.rearrange("(b p) o -> b (p o)", p=P))
+        nc.sync.dma_start(out=v_pool[1][:], in_=vals_planes[:, 1, :])
         nc.sync.dma_start(out=os_sb[:], in_=slot_factor.rearrange("o (p r) -> p (o r)", r=PACK))
-        for t in range(1, PACK):
+        for t in range(2, PACK):
             nc.sync.dma_start(out=v_pool[t][:], in_=vals_planes[:, t, :])
         nc.vector.memset(ident[:], 0.0)
         make_identity(nc, ident[:], nomemset=True)
@@ -88,12 +89,12 @@ def tile_attend_lookahead_read_lean_pl_kernel(
         for b in range(QB):
             for c in range(CHUNKS):
                 a_bank[b, c] = psum.tile([P, BANK], F32, name="bank")
-                first = 2 * BANK * (c % 2)
+                words = k_first[:] if c == 0 else k_rest[:, 2 * BANK * (c - 1) : 2 * BANK * c]
                 nc.tensor.matmul_mx(
                     out=a_bank[b, c][:],
                     lhsT=q_mx[b][0][:].bitcast(FP8X4),
                     lhsT_scale=q_mx[b][1][:],
-                    rhs=k_words[c // 2][:, first : first + 2 * BANK].bitcast(FP4X4),
+                    rhs=words.bitcast(FP4X4),
                     rhs_scale=k_scales[:, BANK * c : BANK * (c + 1)],
                     start=True,
                     stop=True,
@@ -104,11 +105,14 @@ def tile_attend_lookahead_read_lean_pl_kernel(
                 else:
                     nc.scalar.copy(out=dst, in_=a_bank[b, c][:])
 
-        token, follow2, follow3, larger, s_sb = (
+        token, follow2, follow3, larger = (
             [sb.tile([P, I], F32, name=f"{name}{b}", align_bytes=64) for b in range(QB)]
-            for name in ("token", "follow2_", "follow3_", "larger", "s_sb")
+            for name in ("token", "follow2_", "follow3_", "larger")
         )
+        s_sb = [follow2[0], follow2[1]]
         w_bank = {}
+        lam_bank = psum.tile([P, P], F32, name="bank")
+        nc.tensor.transpose(lam_bank[:], lam_rows[:], ident[:])
 
         def turn_values(engine, t, pairs, bank):
             gather(engine, pairs.bitcast(BF16), v_pool[t], list1)
@@ -117,7 +121,7 @@ def tile_attend_lookahead_read_lean_pl_kernel(
 
         def turn_scores(b):
             nc.vector.scalar_tensor_tensor(
-                s_sb[b][:], larger[b][:], lam_sb[:, b : b + 1], token[b][:], ALU.mult, ALU.add
+                s_sb[b][:], larger[b][:], lam_bank[:, b : b + 1], token[b][:], ALU.mult, ALU.add
             )
             w_bank[b] = psum.tile([P, PACK, P], F32, name="bank")
             for r in range(PACK):
@@ -146,9 +150,9 @@ def tile_attend_lookahead_read_lean_pl_kernel(
 
         v_pairs = [sb.tile([P, I // 2], F32, name=f"v_pairs{t}", tag=f"v_pairs{t}", align_bytes=64) for t in (1, 2, 3)]
         v_bank01 = psum.tile([P, 2, 2, P], F32, name="bank")
-        turn_values("vector", 0, follow2[1][:, : I // 2], v_bank01[:, 0])
+        turn_values("vector", 0, follow3[1][:, I // 2 :], v_bank01[:, 0])
         turn_values("scalar", 1, v_pairs[0][:], v_bank01[:, 1])
-        v_bank23 = psum_late.tile([P, 2, 2, P], F32, name="v_bank23", tag="late")
+        v_bank23 = psum.tile([P, 2, 2, P], F32, name="bank")
         turn_values("scalar", 2, v_pairs[1][:], v_bank23[:, 0])
         turn_values("scalar", 3, v_pairs[2][:], v_bank23[:, 1])
         w_grouped = [follow3[1][:, : I // 2].bitcast(BF16), larger[1][:, : I // 2].bitcast(BF16)]
@@ -157,17 +161,14 @@ def tile_attend_lookahead_read_lean_pl_kernel(
         weigh(1, w_grouped[1])
         w_mx0 = quantize("w0", w_grouped[0], P)
         nc.vector.tensor_copy(out=v_grouped[0][:].bitcast(F32), in_=v_bank01[:].rearrange("p t u e -> p t e u"))
-        w_mx1 = quantize("w1", w_grouped[1], P, tag="v_pairs3")
-        v_mx01 = quantize("v01", v_grouped[0][:], 2 * P)
+        w_mx1 = quantize("w1", w_grouped[1], P)
+        v_mx01 = quantize("v01", v_grouped[0][:], 2 * P, tag="v_pairs3")
         nc.scalar.copy(out=v_grouped[1][:].bitcast(F32), in_=v_bank23[:].rearrange("p t u e -> p t e u"))
         v_mx23 = quantize("v23", v_grouped[1][:], 2 * P)
         w_mx = [w_mx0, w_mx1]
         v_mx = [(v_mx01, 0), (v_mx01, P), (v_mx23, 0), (v_mx23, P)]
 
-        o_bank = [
-            psum_late.tile([P, PACK, P], F32, name="o_bank0", tag="late"),
-            psum.tile([P, PACK, P], F32, name="bank"),
-        ]
+        o_bank = [psum.tile([P, PACK, P], F32, name="bank") for b in range(QB)]
         for b in range(QB):
             for t in range(PACK):
                 (codes, scales), first = v_mx[t]

@@ -22,6 +22,7 @@ PACK = 4
 BANK = 512
 QB = Q // P
 CHUNKS = T // BANK
+VECTOR_SHARE = 168
 
 
 def tile_attend_lookahead_read_lean_pl_kernel(
@@ -109,7 +110,7 @@ def tile_attend_lookahead_read_lean_pl_kernel(
             [sb.tile([P, I], F32, name=f"{name}{b}", align_bytes=64) for b in range(QB)]
             for name in ("token", "follow2_", "follow3_", "larger")
         )
-        s_sb = [follow2[0], follow2[1]]
+        s_sb = [follow2[0], follow3[0]]
         w_bank = {}
         lam_bank = psum.tile([P, P], F32, name="bank")
         nc.tensor.transpose(lam_bank[:], lam_rows[:], ident[:])
@@ -150,61 +151,50 @@ def tile_attend_lookahead_read_lean_pl_kernel(
 
         v_pairs = [sb.tile([P, I // 2], F32, name=f"v_pairs{t}", tag=f"v_pairs{t}", align_bytes=64) for t in (1, 2, 3)]
         v_bank01 = psum.tile([P, 2, 2, P], F32, name="bank")
-        turn_values("vector", 0, follow3[1][:, I // 2 :], v_bank01[:, 0])
+        turn_values("vector", 0, follow2[1][:, : I // 2], v_bank01[:, 0])
         turn_values("scalar", 1, v_pairs[0][:], v_bank01[:, 1])
         v_bank23 = psum.tile([P, 2, 2, P], F32, name="bank")
         turn_values("scalar", 2, v_pairs[1][:], v_bank23[:, 0])
         turn_values("scalar", 3, v_pairs[2][:], v_bank23[:, 1])
-        w_grouped = [follow3[1][:, : I // 2].bitcast(BF16), larger[1][:, : I // 2].bitcast(BF16)]
+        w_grouped = follow3[1][:].bitcast(BF16)
         v_grouped = [sb.tile([P, 2 * P * PACK], BF16, name=f"v_grouped{h}", align_bytes=64) for h in range(2)]
-        weigh(0, w_grouped[0])
-        weigh(1, w_grouped[1])
-        w_mx0 = quantize("w0", w_grouped[0], P)
+        weigh(0, w_grouped[:, :I])
+        weigh(1, w_grouped[:, I:])
         nc.vector.tensor_copy(out=v_grouped[0][:].bitcast(F32), in_=v_bank01[:].rearrange("p t u e -> p t e u"))
-        w_mx1 = quantize("w1", w_grouped[1], P)
+        w_codes, w_scales = quantize("w", w_grouped, Q)
         v_mx01 = quantize("v01", v_grouped[0][:], 2 * P, tag="v_pairs3")
         nc.scalar.copy(out=v_grouped[1][:].bitcast(F32), in_=v_bank23[:].rearrange("p t u e -> p t e u"))
         v_mx23 = quantize("v23", v_grouped[1][:], 2 * P)
-        w_mx = [w_mx0, w_mx1]
         v_mx = [(v_mx01, 0), (v_mx01, P), (v_mx23, 0), (v_mx23, P)]
 
-        o_bank = [psum.tile([P, PACK, P], F32, name="bank") for b in range(QB)]
-        for b in range(QB):
-            for t in range(PACK):
-                (codes, scales), first = v_mx[t]
-                nc.tensor.matmul_mx(
-                    out=o_bank[b][:, t, :],
-                    lhsT=codes[:, first : first + P].bitcast(FP8X4),
-                    lhsT_scale=scales[:, first : first + P],
-                    rhs=w_mx[b][0][:].bitcast(FP8X4),
-                    rhs_scale=w_mx[b][1][:],
-                    start=True,
-                    stop=True,
-                )
-
-        out_planes = out_0.rearrange("(p t) q -> p t q", t=PACK)
-        o_grouped = sb.tile([P, Q, PACK], BF16, name="o_grouped", align_bytes=64)
-        o_sb = [sb.tile([P, PACK, P], F32, name=f"o_sb{b}") for b in range(QB)]
-        o_codes = sb.tile([P, Q], U32, name="o_codes", align_bytes=64)
-        o_scales = sb.tile([P, Q], U8, name="o_scales", align_bytes=64)
-
-        def store_result(b):
-            nc.scalar.copy(out=o_sb[b][:], in_=o_bank[b][:])
-            nc.sync.dma_start(out=out_planes[:, :, P * b : P * (b + 1)], in_=o_sb[b][:])
-
-        def quantize_result(b, source):
-            cols = slice(P * b, P * (b + 1))
-            nc.vector.tensor_copy(out=o_grouped[:, cols, :], in_=source[:].rearrange("p t q -> p q t"))
-            nc.vector.quantize_mx(
-                out=o_codes[:, cols].bitcast(FP8X4),
-                scales=o_scales[:, cols],
-                in_=o_grouped[:, cols, :].rearrange("p q t -> p (q t)"),
+        o_bank01 = psum.tile([P, 2, Q], F32, name="bank")
+        o_bank2 = psum.tile([P, Q], F32, name="bank")
+        o_bank3 = psum.tile([P, Q], F32, name="bank")
+        o_plane = [o_bank01[:, 0, :], o_bank01[:, 1, :], o_bank2[:], o_bank3[:]]
+        for t in range(PACK):
+            (codes, scales), first = v_mx[t]
+            nc.tensor.matmul_mx(
+                out=o_plane[t],
+                lhsT=codes[:, first : first + P].bitcast(FP8X4),
+                lhsT_scale=scales[:, first : first + P],
+                rhs=w_codes[:].bitcast(FP8X4),
+                rhs_scale=w_scales[:],
+                start=True,
+                stop=True,
             )
 
-        quantize_result(0, o_bank[0])
-        store_result(1)
-        store_result(0)
-        quantize_result(1, o_sb[1])
+        out_planes = out_0.rearrange("(p t) q -> p t q", t=PACK)
+        o_sb = sb.tile([P, PACK, Q], F32, name="o_sb")
+        nc.scalar.copy(out=o_sb[:, 0:2, :], in_=o_bank01[:])
+        nc.sync.dma_start(out=out_planes[:, 0:2, :], in_=o_sb[:, 0:2, :])
+        nc.vector.tensor_copy(out=o_sb[:, 2, :], in_=o_bank2[:])
+        nc.scalar.copy(out=o_sb[:, 3, :], in_=o_bank3[:])
+        nc.sync.dma_start(out=out_planes[:, 2:4, :], in_=o_sb[:, 2:4, :])
+        o_grouped = sb.tile([P, Q, PACK], BF16, name="o_grouped", align_bytes=64)
+        o_view = o_sb[:].rearrange("p t q -> p q t")
+        nc.vector.tensor_copy(out=o_grouped[:, :VECTOR_SHARE, :], in_=o_view[:, :VECTOR_SHARE, :])
+        nc.scalar.copy(out=o_grouped[:, VECTOR_SHARE:, :], in_=o_view[:, VECTOR_SHARE:, :])
+        o_codes, o_scales = quantize("o", o_grouped[:].rearrange("p q t -> p (q t)"), Q)
         nc.sync.dma_start(out=out_1[0].rearrange("p c r -> p (c r)").bitcast(I32), in_=o_codes[:].bitcast(I32))
         for row in range(4):
             queue = nc.scalar if row % 2 == 0 else nc.sync

from contextlib import ExitStack

import concourse.mybir as mybir
from concourse.masks import make_identity

D, T, I, Q, E = 512, 2048, 512, 256, 512
FLOPS = 2 * D * Q * T + 2 * I * E * Q

F32 = mybir.dt.float32
BF16 = mybir.dt.bfloat16
I32 = mybir.dt.int32
U32 = mybir.dt.uint32
U16 = mybir.dt.uint16
U8 = mybir.dt.uint8
FP8X4 = mybir.dt.float8_e4m3fn_x4
FP4X4 = mybir.dt.float4_e2m1fn_x4
ALU = mybir.AluOpType
COPY = mybir.ActivationFunctionType.Copy

P = 128
PACK = 4
BANK = 512
QB = Q // P
CHUNKS = T // BANK
VECTOR_SHARE = 168


def tile_attend_lookahead_read_lean_pl_kernel(
    tc, query, keys_words, keys_scales, lam, slot_factor, vals, offs, offs2, offs3, out_0, out_1, out_2
):
    nc = tc.nc
    with ExitStack() as ctx:
        sb = ctx.enter_context(tc.tile_pool(name="sb", bufs=1))
        psum = ctx.enter_context(tc.psum_pool(name="psum", bufs=8))

        list1 = sb.tile([P, I // 16], U16, name="list1")
        list2 = sb.tile([P, I // 16], U16, name="list2")
        list3 = sb.tile([P, I // 16], U16, name="list3")
        q_raw = sb.tile([P, PACK, Q], F32, name="q_raw")
        k_first = sb.tile([P, 2 * BANK], U8, name="k_first", align_bytes=64)
        k_rest = sb.tile([P, 2 * (T - BANK)], U8, name="k_rest", align_bytes=64)
        k_scales = sb.tile([P, T], U8, name="k_scales", align_bytes=64)
        lam_rows = sb.tile([P, P], F32, name="lam_rows")
        os_sb = sb.tile([P, PACK], F32, name="os_sb")
        ident = sb.tile([P, P], F32, name="ident")
        v_pool = [sb.tile([P, T], F32, name=f"v_pool{t}") for t in range(PACK)]
        a_sb = [sb.tile([P, T], F32, name=f"a_sb{b}") for b in range(QB)]

        nc.vector.memset(k_scales[:].bitcast(I32), 0)
        vals_planes = vals.rearrange("(p t) c -> p t c", t=PACK)
        nc.sync.dma_start(out=q_raw[:], in_=query.rearrange("(p j) q -> p j q", j=PACK))
        nc.sync.dma_start(out=k_first[:].bitcast(I32), in_=keys_words[0, :, : 2 * BANK].bitcast(I32))
        nc.sync.dma_start(list2[:], offs2)
        for row in range(4):
            nc.sync.dma_start(
                out=k_scales[row:P:32, :].bitcast(I32), in_=keys_scales[0, row:16:4, :].bitcast(I32)
            )
        nc.sync.dma_start(out=k_rest[:].bitcast(I32), in_=keys_words[0, :, 2 * BANK :].bitcast(I32))
        nc.sync.dma_start(out=v_pool[0][:], in_=vals_planes[:, 0, :])
        nc.sync.dma_start(list3[:], offs3)
        nc.sync.dma_start(list1[:], offs)
        nc.vector.memset(lam_rows[:], 0.0)
        nc.sync.dma_start(out=lam_rows[:QB, :], in_=lam.rearrange("(b p) o -> b (p o)", p=P))
        nc.sync.dma_start(out=v_pool[1][:], in_=vals_planes[:, 1, :])
        nc.sync.dma_start(out=os_sb[:], in_=slot_factor.rearrange("o (p r) -> p (o r)", r=PACK))
        for t in range(2, PACK):
            nc.sync.dma_start(out=v_pool[t][:], in_=vals_planes[:, t, :])
        nc.vector.memset(ident[:], 0.0)
        make_identity(nc, ident[:], nomemset=True)

        def quantize(name, grouped, width, tag=""):
            codes = sb.tile([P, width], U32, name=name + "_codes", tag=tag, align_bytes=64)
            scales = sb.tile([P, width], U8, name=name + "_scales", align_bytes=64)
            nc.vector.quantize_mx(out=codes[:].bitcast(FP8X4), scales=scales[:], in_=grouped)
            return codes, scales

        def gather(engine, dst, window, offsets):
            if engine == "vector":
                nc.vector.tensor_copy(dst, window[:].indirect(offsets[:]))
            else:
                nc.scalar.activation(dst, window[:].indirect(offsets[:]), COPY)

        q_grouped = [sb.tile([P, P, PACK], BF16, name=f"q_grouped{b}", align_bytes=64) for b in range(QB)]
        q_view = q_raw[:].rearrange("p j q -> p q j")
        nc.vector.tensor_copy(out=q_grouped[0][:], in_=q_view[:, 0:P, :])
        nc.scalar.copy(out=q_grouped[1][:], in_=q_view[:, P : 2 * P, :])
        q_mx = [quantize(f"q{b}", q_grouped[b][:].rearrange("p q j -> p (q j)"), P) for b in range(QB)]

        a_bank = {}
        for b in range(QB):
            for c in range(CHUNKS):
                a_bank[b, c] = psum.tile([P, BANK], F32, name="bank")
                words = k_first[:] if c == 0 else k_rest[:, 2 * BANK * (c - 1) : 2 * BANK * c]
                nc.tensor.matmul_mx(
                    out=a_bank[b, c][:],
                    lhsT=q_mx[b][0][:].bitcast(FP8X4),
                    lhsT_scale=q_mx[b][1][:],
                    rhs=words.bitcast(FP4X4),
                    rhs_scale=k_scales[:, BANK * c : BANK * (c + 1)],
                    start=True,
                    stop=True,
                )
                dst = a_sb[b][:, BANK * c : BANK * (c + 1)]
                if c % 2 == 1 and (b, c) != (QB - 1, CHUNKS - 1):
                    nc.vector.tensor_copy(out=dst, in_=a_bank[b, c][:])
                else:
                    nc.scalar.copy(out=dst, in_=a_bank[b, c][:])

        token, follow2, follow3, larger = (
            [sb.tile([P, I], F32, name=f"{name}{b}", align_bytes=64) for b in range(QB)]
            for name in ("token", "follow2_", "follow3_", "larger")
        )
        s_sb = [follow2[0], follow3[0]]
        w_bank = {}
        lam_bank = psum.tile([P, P], F32, name="bank")
        nc.tensor.transpose(lam_bank[:], lam_rows[:], ident[:])

        def turn_values(engine, t, pairs, bank):
            gather(engine, pairs.bitcast(BF16), v_pool[t], list1)
            for u in range(2):
                nc.tensor.transpose(bank[:, u, :], pairs[:, u::2], ident[:])

        def turn_scores(b):
            nc.vector.scalar_tensor_tensor(
                s_sb[b][:], larger[b][:], lam_bank[:, b : b + 1], token[b][:], ALU.mult, ALU.add
            )
            w_bank[b] = psum.tile([P, PACK, P], F32, name="bank")
            for r in range(PACK):
                nc.tensor.transpose(w_bank[b][:, r, :], s_sb[b][:, r::PACK], ident[:])

        def weigh(b, grouped):
            nc.vector.scalar_tensor_tensor(
                grouped.rearrange("p (q r) -> p q r", r=PACK),
                w_bank[b][:].rearrange("p r q -> p q r"),
                0.0,
                os_sb[:].unsqueeze(1).to_broadcast([P, P, PACK]),
                ALU.max,
                ALU.mult,
            )

        gather("vector", follow2[0][:], a_sb[0], list2)
        gather("vector", follow3[0][:], a_sb[0], list3)
        nc.vector.tensor_tensor(larger[0][:], follow2[0][:], follow3[0][:], ALU.max)
        gather("vector", token[0][:], a_sb[0], list1)
        turn_scores(0)
        gather("scalar", follow2[1][:], a_sb[1], list2)
        gather("scalar", follow3[1][:], a_sb[1], list3)
        gather("scalar", token[1][:], a_sb[1], list1)
        nc.vector.tensor_tensor(larger[1][:], follow2[1][:], follow3[1][:], ALU.max)
        turn_scores(1)

        v_pairs = [sb.tile([P, I // 2], F32, name=f"v_pairs{t}", tag=f"v_pairs{t}", align_bytes=64) for t in (1, 2, 3)]
        v_bank01 = psum.tile([P, 2, 2, P], F32, name="bank")
        turn_values("vector", 0, follow2[1][:, : I // 2], v_bank01[:, 0])
        turn_values("scalar", 1, v_pairs[0][:], v_bank01[:, 1])
        v_bank23 = psum.tile([P, 2, 2, P], F32, name="bank")
        turn_values("scalar", 2, v_pairs[1][:], v_bank23[:, 0])
        turn_values("scalar", 3, v_pairs[2][:], v_bank23[:, 1])
        w_grouped = follow3[1][:].bitcast(BF16)
        v_grouped = [sb.tile([P, 2 * P * PACK], BF16, name=f"v_grouped{h}", align_bytes=64) for h in range(2)]
        weigh(0, w_grouped[:, :I])
        weigh(1, w_grouped[:, I:])
        nc.vector.tensor_copy(out=v_grouped[0][:].bitcast(F32), in_=v_bank01[:].rearrange("p t u e -> p t e u"))
        w_codes, w_scales = quantize("w", w_grouped, Q)
        v_mx01 = quantize("v01", v_grouped[0][:], 2 * P, tag="v_pairs3")
        nc.scalar.copy(out=v_grouped[1][:].bitcast(F32), in_=v_bank23[:].rearrange("p t u e -> p t e u"))
        v_mx23 = quantize("v23", v_grouped[1][:], 2 * P)
        v_mx = [(v_mx01, 0), (v_mx01, P), (v_mx23, 0), (v_mx23, P)]

        o_bank01 = psum.tile([P, 2, Q], F32, name="bank")
        o_bank2 = psum.tile([P, Q], F32, name="bank")
        o_bank3 = psum.tile([P, Q], F32, name="bank")
        o_plane = [o_bank01[:, 0, :], o_bank01[:, 1, :], o_bank2[:], o_bank3[:]]
        for t in range(PACK):
            (codes, scales), first = v_mx[t]
            nc.tensor.matmul_mx(
                out=o_plane[t],
                lhsT=codes[:, first : first + P].bitcast(FP8X4),
                lhsT_scale=scales[:, first : first + P],
                rhs=w_codes[:].bitcast(FP8X4),
                rhs_scale=w_scales[:],
                start=True,
                stop=True,
            )

        out_planes = out_0.rearrange("(p t) q -> p t q", t=PACK)
        o_sb = sb.tile([P, PACK, Q], F32, name="o_sb")
        nc.scalar.copy(out=o_sb[:, 0:2, :], in_=o_bank01[:])
        nc.sync.dma_start(out=out_planes[:, 0:2, :], in_=o_sb[:, 0:2, :])
        nc.vector.tensor_copy(out=o_sb[:, 2, :], in_=o_bank2[:])
        nc.scalar.copy(out=o_sb[:, 3, :], in_=o_bank3[:])
        nc.sync.dma_start(out=out_planes[:, 2:4, :], in_=o_sb[:, 2:4, :])
        o_grouped = sb.tile([P, Q, PACK], BF16, name="o_grouped", align_bytes=64)
        o_view = o_sb[:].rearrange("p t q -> p q t")
        nc.vector.tensor_copy(out=o_grouped[:, :VECTOR_SHARE, :], in_=o_view[:, :VECTOR_SHARE, :])
        nc.scalar.copy(out=o_grouped[:, VECTOR_SHARE:, :], in_=o_view[:, VECTOR_SHARE:, :])
        o_codes, o_scales = quantize("o", o_grouped[:].rearrange("p q t -> p (q t)"), Q)
        nc.sync.dma_start(out=out_1[0].rearrange("p c r -> p (c r)").bitcast(I32), in_=o_codes[:].bitcast(I32))
        for row in range(4):
            queue = nc.scalar if row % 2 == 0 else nc.sync
            queue.dma_start(out=out_2[0, row:16:4, :].bitcast(I32), in_=o_scales[row:P:32, :].bitcast(I32))
